import numpy as np
import ml_dtypes


def mxq(x, axis, fmt="e4m3"):
    dtype, down = {"e4m3": (ml_dtypes.float8_e4m3fn, 7), "e5m2": (ml_dtypes.float8_e5m2, 14)}[fmt]
    v = np.moveaxis(np.asarray(x, np.float32).astype(ml_dtypes.bfloat16).astype(np.float64), axis, -1)
    blocks = v.reshape(v.shape[:-1] + (-1, 32))
    amax = np.abs(blocks).max(-1, keepdims=True)
    byte = np.maximum(np.where(amax > 0, np.frexp(amax)[1] - 1 + 127, 0) - down, 1)
    scale = np.exp2(byte - 127.0)
    codes = (blocks / scale).astype(np.float32).astype(dtype).astype(np.float64)
    return np.moveaxis((codes * scale).reshape(v.shape), -1, axis)


WIDE = False


def mx_kscale(k):
    if not WIDE:
        return np.ones(k)
    levels = np.array([10, -10, 5, -5, 0])
    if k % 512:
        return np.exp2(np.random.permutation(np.resize(levels, k // 32))).repeat(32)
    a = np.empty((k // 512, 16))
    for p in range(k // 512):
        a[p, :8] = np.random.permutation(np.resize(levels, 8))
        for g in range(8):
            far = levels[np.abs(levels - a[p, g]) >= 10]
            a[p, g + 8] = far[np.random.randint(len(far))]
    return np.exp2(a.ravel()).repeat(32)


def f64(x):
    return np.asarray(x).astype(np.float64)


def striped(idx):
    return np.tile(np.asarray(idx).reshape(-1, 16).T, (8, 1)).astype(np.uint16)


def unstriped(offs):
    return offs[:16].T.reshape(-1).astype(np.int64)


def striped8(idx):
    return np.asarray(idx).reshape(8, -1, 16).transpose(0, 2, 1).reshape(128, -1).astype(np.uint16)


def unstriped8(offs):
    return offs.reshape(8, 16, -1).transpose(0, 2, 1).reshape(8, -1).astype(np.int64)


def pick8(x, idx, run):
    r = np.arange(len(x))
    return x[r[:, None], idx[r % (8 * run) // run]]


E2M1 = np.array([0.0, 0.5, 1.0, 1.5, 2.0, 3.0, 4.0, 6.0, -0.0, -0.5, -1.0, -1.5, -2.0, -3.0, -4.0, -6.0])


def pack_weight(w, fmt):
    k, n = w.shape
    w = f64(np.asarray(w, np.float32).astype(ml_dtypes.bfloat16)).reshape(k // 32, 32, n)
    amax = np.abs(w).max(1)
    if fmt == "e4m3":
        byte = np.frexp(amax)[1] - 1 + 127 - 7
    else:
        mant, ex = np.frexp(amax / 6.0)
        byte = np.where(mant > 0.5, ex, ex - 1) + 127
    byte = np.clip(np.where(amax > 0, byte, 1), 1, 254)
    scaled = (w * np.exp2(127.0 - byte)[:, None, :]).reshape(k, n).astype(np.float32)
    by_word = np.ascontiguousarray(scaled.reshape(k // 512, 128, 4, n).transpose(0, 1, 3, 2))
    if fmt == "e4m3":
        words = by_word.astype(ml_dtypes.float8_e4m3fn).view(np.uint8)
    else:
        c = by_word.astype(ml_dtypes.float4_e2m1fn).view(np.uint8) & 0xF
        words = (c[..., 0::2] | (c[..., 1::2] << 4)).reshape(k // 512, 128, 2 * n)
    return np.ascontiguousarray(words), np.ascontiguousarray(byte.astype(np.uint8).reshape(k // 512, 16, n))


def unpack_weight(words, scales, fmt):
    g, _, n = scales.shape
    words = np.ascontiguousarray(words).reshape(g, 128, n, -1)
    if fmt == "e4m3":
        vals = words.view(ml_dtypes.float8_e4m3fn).astype(np.float64)
    else:
        nib = np.empty((g, 128, n, 4), np.uint8)
        nib[..., 0::2] = words & 0xF
        nib[..., 1::2] = words >> 4
        vals = E2M1[nib]
    vals = vals * np.repeat(np.exp2(scales.astype(np.float64) - 127.0), 8, axis=1)[..., None]
    return vals.transpose(0, 1, 3, 2).reshape(g * 512, n)


K, J, R, T, Z, M, O, C, D, N, S = 512, 512, 512, 2048, 512, 1024, 256, 1024, 1024, 256, 1024


def setup_inputs():
    n = np.random.standard_normal
    idx = np.random.permutation(T)[:J]
    idx2 = np.random.permutation(M)[:J]
    idx3 = np.stack([np.random.permutation(C)[:J] for _ in range(8)])
    idx4 = np.stack([np.random.permutation(C)[:J] for _ in range(8)])
    idx5 = np.stack([np.random.permutation(D)[:J] for _ in range(8)])
    idx6 = np.stack([np.random.permutation(D)[:O] for _ in range(8)])
    idx7 = np.random.permutation(S)[:N]
    fk = mx_kscale(K)
    fr = mx_kscale(R)
    fz = mx_kscale(Z)
    xtp = pack_weight(n((K, T)) * fk[:, None], "e2m1")
    wp = pack_weight(n((K, R)) * 1 / np.sqrt(K) / fk[:, None] * fr, "e4m3")
    xop = pack_weight(n((Z, M)) / fz[:, None], "e2m1")
    w2p = pack_weight(n((Z, R)) * 1 / np.sqrt(Z) * fz[:, None] * fr, "e4m3")
    vsp = pack_weight(n((R, S)) * 1 / np.sqrt(R) / fr[:, None], "e4m3")
    return {
        "xt_words": xtp[0],
        "xt_scales": xtp[1],
        "w_words": wp[0],
        "w_scales": wp[1],
        "xo_words": xop[0],
        "xo_scales": xop[1],
        "w2_words": w2p[0],
        "w2_scales": w2p[1],
        "sa": (np.random.uniform(0.5, 1.6, (R, 1))).astype(np.float32),
        "sb": (np.random.uniform(0.5, 1.6, (R, 1))).astype(np.float32),
        "vs_words": vsp[0],
        "vs_scales": vsp[1],
        "offs": striped(idx),
        "offs2": striped(idx2),
        "offs3": striped8(idx3),
        "offs4": striped8(idx4),
        "offs5": striped8(idx5),
        "offs6": striped8(idx6),
        "offs7": striped(idx7),
    }


def reference(xt_words, xt_scales, w_words, w_scales, xo_words, xo_scales, w2_words, w2_scales, sa, sb, vs_words, vs_scales, offs, offs2, offs3, offs4, offs5, offs6, offs7):
    idx = unstriped(offs)
    idx2 = unstriped(offs2)
    idx3 = unstriped8(offs3)
    idx4 = unstriped8(offs4)
    idx5 = unstriped8(offs5)
    idx6 = unstriped8(offs6)
    idx7 = unstriped(offs7)
    xtu = unpack_weight(xt_words, xt_scales, "e2m1")
    wu = unpack_weight(w_words, w_scales, "e4m3")
    xou = unpack_weight(xo_words, xo_scales, "e2m1")
    w2u = unpack_weight(w2_words, w2_scales, "e4m3")
    vsu = unpack_weight(vs_words, vs_scales, "e4m3")
    xtidxg = xtu[:, idx]
    a = wu.T @ xtidxg
    xoidx2g = xou[:, idx2]
    b = w2u.T @ xoidx2g
    pw = np.zeros((R, C))
    pw[np.arange(R)[:, None], idx3[np.arange(R) % 512 // 64]] = a
    h1 = b - pick8(pw, idx4, 64) * f64(sa)
    pv = np.zeros((R, D))
    pv[np.arange(R)[:, None], idx5[np.arange(R) % 512 // 64]] = h1
    g1 = np.maximum(pv, 0.0)
    hid = pick8(g1, idx6, 64) * f64(sb)
    vsidx7g = vsu[:, idx7]
    hidq = mxq(hid, 0, "e4m3")
    y = vsidx7g.T @ hidq
    return y

@@ -1,0 +1,236 @@
+from contextlib import ExitStack
+
+import concourse.mybir as mybir
+
+K, J, R, T, M, O, C, N, S = 512, 512, 512, 2048, 1024, 256, 1024, 256, 1024
+FLOPS = 2 * (K * R * J + K * R * J + R * N * O)
+
+F32 = mybir.dt.float32
+BF16 = mybir.dt.bfloat16
+I32 = mybir.dt.int32
+U32 = mybir.dt.uint32
+U16 = mybir.dt.uint16
+U8 = mybir.dt.uint8
+FP8X4 = mybir.dt.float8_e4m3fn_x4
+FP4X4 = mybir.dt.float4_e2m1fn_x4
+COPY = mybir.ActivationFunctionType.Copy
+SUBTRACT = mybir.AluOpType.subtract
+
+P = 128
+PACK = 4
+QUADS = 4
+HALF = J // 2
+
+
+def tile_picked_tokens_plain_two_deltapost_store_plain_kernel(
+    tc, xt_words, xt_scales, w_words, w_scales, xo_words, xo_scales, w2_words, w2_scales,
+    sa, sb, vs_words, vs_scales, offs, offs2, offs3, offs4, offs5, offs6, offs7, out,
+):
+    nc = tc.nc
+    with ExitStack() as ctx:
+        keep = ctx.enter_context(tc.tile_pool(name="keep", bufs=1))
+        psum = ctx.enter_context(tc.psum_pool(name="psum", bufs=4))
+
+        def load_list(src, name):
+            tile = keep.tile(list(src.shape), U16, name=name)
+            nc.sync.dma_start(tile[:], src)
+            return tile
+
+        def load_table_scales(src, width, name, clear):
+            window = keep.tile([P, width], U8, name=name, tag="scale_window", align_bytes=64)
+            clear.memset(window[:].bitcast(I32), 0)
+            rows = src[0].bitcast(I32)
+            for q in range(QUADS):
+                nc.sync.dma_start(window[32 * q : 32 * q + 4, :].bitcast(I32), rows[4 * q : 4 * q + 4, :])
+            return window
+
+        def load_table_words(src, width, dtype, name):
+            window = keep.tile([P, width], dtype, name=name, tag="word_window", align_bytes=64)
+            nc.sync.dma_start(window[:].bitcast(I32), src.bitcast(I32))
+            return window
+
+        def load_weight_words(words, name):
+            raw_words = keep.tile([P, R], I32, name=name + "_raw_words", tag="raw_words")
+            nc.sync.dma_start(raw_words[:], words[0].rearrange("p c t -> p (c t)").bitcast(I32))
+            return raw_words
+
+        def load_weight_scales(scales, name):
+            staged = keep.tile([4, QUADS, R // 4], I32, name=name + "_staged", tag="staged")
+            nc.sync.dma_start(staged[:], scales[0].bitcast(I32).rearrange("(q i) n -> i q n", i=4))
+            raw_scales = keep.tile([P, R], U8, name=name + "_raw_scales", tag="raw_scales")
+            nc.vector.memset(raw_scales[:].bitcast(I32), 0)
+            for q in range(QUADS):
+                nc.vector.tensor_copy(raw_scales[32 * q : 32 * q + 4, :].bitcast(I32), staged[:, q, :])
+            return raw_scales
+
+        def deal(dealt, raw, first, last):
+            nc.vector.tensor_copy(
+                dealt[:, first * P : last * P].rearrange("p (t m) -> p t m", m=P),
+                raw[:].rearrange("p (m t) -> p t m", t=PACK)[:, first:last, :],
+            )
+
+        token_list = load_list(offs, "token_list")
+        xt_scale_window = load_table_scales(xt_scales, T, "xt_scale_window", nc.gpsimd)
+        w_raw_scales = load_weight_scales(w_scales, "w")
+        xt_word_window = load_table_words(xt_words[0], T, U16, "xt_word_window")
+        w_raw_words = load_weight_words(w_words, "w")
+        put_first_list = load_list(offs3, "put_first_list")
+
+        first_boards = [keep.tile([P, C], F32, name="first_board%d" % i) for i in range(2)]
+        for board in first_boards:
+            nc.vector.memset(board[:], 0.0)
+
+        w_dealt_words = keep.tile([P, R], I32, align_bytes=64)
+        w_dealt_scales = keep.tile([P, R], U8, align_bytes=64)
+        a_rows = [keep.tile([P, J], F32, name="a_rows%d" % t, tag="rows%d" % t) for t in range(PACK)]
+
+        def put_first(t, slots):
+            nc.scalar.activation(
+                first_boards[t % 2][:].indirect(put_first_list[:, slots.start // 16 : slots.stop // 16]),
+                a_rows[t][:, slots],
+                COPY,
+            )
+
+        deal(w_dealt_scales, w_raw_scales, 0, 1)
+        for h in range(2):
+            slots = slice(h * HALF, (h + 1) * HALF)
+            entries = token_list[:, slots.start // 16 : slots.stop // 16]
+            token_scales = keep.tile([P, HALF], U8, align_bytes=64)
+            token_words = keep.tile([P, HALF], U16, align_bytes=64)
+            nc.vector.tensor_copy(token_scales[:], xt_scale_window[:].indirect(entries))
+            nc.vector.tensor_copy(token_words[:], xt_word_window[:].indirect(entries))
+            for t in range(PACK):
+                if h == 0 and t < 2:
+                    deal(w_dealt_words, w_raw_words, t, 1 if t == 0 else PACK)
+                if h == 0 and t == 1:
+                    deal(w_dealt_scales, w_raw_scales, 1, PACK)
+                acc = psum.tile([P, J], F32, name="acc", tag="acc")
+                nc.tensor.matmul_mx(
+                    out=acc[:, :HALF],
+                    lhsT=w_dealt_words[:, t * P : (t + 1) * P].bitcast(FP8X4),
+                    lhsT_scale=w_dealt_scales[:, t * P : (t + 1) * P],
+                    rhs=token_words[:].bitcast(FP4X4),
+                    rhs_scale=token_scales[:],
+                    start=True,
+                    stop=True,
+                )
+                if h == 0 and t == 0:
+                    nc.scalar.activation(a_rows[t][:, slots], acc[:, :HALF], COPY)
+                else:
+                    nc.vector.tensor_copy(a_rows[t][:, slots], acc[:, :HALF])
+                if t < 2:
+                    put_first(t, slots)
+        all_slots = slice(0, J)
+
+        read_first_list = load_list(offs4, "read_first_list")
+        first_weights = keep.tile([P, PACK], F32)
+        nc.sync.dma_start(first_weights[:], sa.rearrange("(p t) o -> p (t o)", t=PACK))
+        note_list = load_list(offs2, "note_list")
+        put_second_list = load_list(offs5, "put_second_list")
+        read_second_list = load_list(offs6, "read_second_list")
+        second_weights = keep.tile([P, PACK], F32)
+        nc.sync.dma_start(second_weights[:], sb.rearrange("(p t) o -> p (t o)", t=PACK))
+        store_list = load_list(offs7, "store_list")
+
+        xo_scale_window = load_table_scales(xo_scales, M, "xo_scale_window", nc.vector)
+        xo_word_window = load_table_words(xo_words[0], M, U16, "xo_word_window")
+        w2_raw_scales = load_weight_scales(w2_scales, "w2")
+        w2_raw_words = load_weight_words(w2_words, "w2")
+        w2_dealt_words = keep.tile([P, R], I32, align_bytes=64)
+        w2_dealt_scales = keep.tile([P, R], U8, align_bytes=64)
+        deal(w2_dealt_scales, w2_raw_scales, 0, PACK)
+        deal(w2_dealt_words, w2_raw_words, 0, PACK)
+        note_words = keep.tile([P, J], U16, align_bytes=64)
+        note_scales = keep.tile([P, J], U8, align_bytes=64)
+        nc.vector.tensor_copy(note_scales[:], xo_scale_window[:].indirect(note_list[:]))
+        nc.vector.tensor_copy(note_words[:], xo_word_window[:].indirect(note_list[:]))
+        b_rows = []
+        for t in range(PACK):
+            b_acc = psum.tile([P, J], F32, name="b_acc", tag="b_acc")
+            nc.tensor.matmul_mx(
+                out=b_acc[:],
+                lhsT=w2_dealt_words[:, t * P : (t + 1) * P].bitcast(FP8X4),
+                lhsT_scale=w2_dealt_scales[:, t * P : (t + 1) * P],
+                rhs=note_words[:].bitcast(FP4X4),
+                rhs_scale=note_scales[:],
+                start=True,
+                stop=True,
+            )
+            b_rows.append(b_acc)
+
+        taken = [keep.tile([P, J], F32, name="taken%d" % t) for t in range(PACK)]
+        difference = [keep.tile([P, J], F32, name="difference%d" % t) for t in range(PACK)]
+        positive = [keep.tile([P, J], F32, name="positive%d" % t) for t in range(PACK)]
+        hid_rows = keep.tile([P, PACK * O], BF16, align_bytes=64)
+        hid_grouped = [keep.tile([P, P * PACK], BF16, name="hid_grouped%d" % g, align_bytes=64) for g in range(2)]
+
+        def read_first(t):
+            nc.scalar.activation(
+                taken[t][:], first_boards[t % 2][:].indirect(read_first_list[:]), COPY,
+                scale=first_weights[:, t : t + 1],
+            )
+            nc.vector.tensor_tensor(difference[t][:], b_rows[t][:], taken[t][:], SUBTRACT)
+            nc.vector.tensor_scalar_max(positive[t][:], difference[t][:], 0.0)
+
+        second_boards = []
+
+        def put_second(t):
+            if t < 2:
+                board = keep.tile([P, C], F32, name="second_board%d" % t, tag="rows%d" % t)
+                nc.vector.memset(board[:], 0.0)
+                second_boards.append(board)
+            nc.scalar.activation(second_boards[t % 2][:].indirect(put_second_list[:]), positive[t][:], COPY)
+
+        def read_second(t):
+            nc.scalar.activation(
+                hid_rows[:, t * O : (t + 1) * O], second_boards[t % 2][:].indirect(read_second_list[:]), COPY,
+                scale=second_weights[:, t : t + 1],
+            )
+            for g in range(2):
+                nc.vector.tensor_copy(
+                    hid_grouped[g][:].rearrange("p (o t) -> p o t", t=PACK)[:, :, t],
+                    hid_rows[:, t * O + g * P : t * O + (g + 1) * P],
+                )
+
+        for step in range(1, PACK + 3):
+            if 2 <= step < PACK:
+                put_first(step, all_slots)
+            if step - 1 < PACK:
+                read_first(step - 1)
+            if 0 <= step - 2 < PACK:
+                put_second(step - 2)
+            if 0 <= step - 3 < PACK:
+                read_second(step - 3)
+
+        vs_scale_window = load_table_scales(vs_scales, S, "vs_scale_window", nc.vector)
+        vs_word_window = load_table_words(vs_words[0].rearrange("p c t -> p (c t)"), S, U32, "vs_word_window")
+        store_words = keep.tile([P, N], U32, align_bytes=64)
+        store_scales = keep.tile([P, N], U8, align_bytes=64)
+        nc.vector.tensor_copy(store_scales[:], vs_scale_window[:].indirect(store_list[:]))
+        nc.vector.tensor_copy(store_words[:], vs_word_window[:].indirect(store_list[:]))
+
+        for g in range(2):
+            hid_words = keep.tile([P, P], U32, name="hid_words%d" % g, align_bytes=64)
+            hid_scales = keep.tile([P, P], U8, name="hid_scales%d" % g, align_bytes=64)
+            nc.vector.quantize_mx(out=hid_words[:].bitcast(FP8X4), scales=hid_scales[:], in_=hid_grouped[g][:])
+            y_acc = psum.tile([P, J], F32, name="y_acc", tag="acc")
+            for half in range(N // P):
+                features = slice(half * P, (half + 1) * P)
+                nc.tensor.matmul_mx(
+                    out=y_acc[:, features],
+                    lhsT=store_words[:, features].bitcast(FP8X4),
+                    lhsT_scale=store_scales[:, features],
+                    rhs=hid_words[:].bitcast(FP8X4),
+                    rhs_scale=hid_scales[:],
+                    start=True,
+                    stop=True,
+                )
+            y_rows = keep.tile([P, N], F32, name="y_rows%d" % g)
+            if g == 0:
+                nc.scalar.copy(y_rows[:], y_acc[:, :N])
+            else:
+                nc.vector.tensor_copy(y_rows[:], y_acc[:, :N])
+            nc.sync.dma_start(
+                out.rearrange("(h p) o -> p h o", p=P)[:, :, g * P : (g + 1) * P],
+                y_rows[:].rearrange("p (h o) -> p h o", o=P),
+            )

@@ -36,12 +36,14 @@ def tile_picked_tokens_plain_two_deltapost_store_plain_kernel(
             nc.sync.dma_start(tile[:], src)
             return tile
 
-        def load_table_scales(src, width, name, clear):
+        def load_table_scales(src, width, name, clears, queue):
             window = keep.tile([P, width], U8, name=name, tag="scale_window", align_bytes=64)
-            clear.memset(window[:].bitcast(I32), 0)
+            share = width // len(clears)
+            for i, clear in enumerate(clears):
+                clear.memset(window[:, i * share : (i + 1) * share].bitcast(I32), 0)
             rows = src[0].bitcast(I32)
             for q in range(QUADS):
-                nc.sync.dma_start(window[32 * q : 32 * q + 4, :].bitcast(I32), rows[4 * q : 4 * q + 4, :])
+                queue.dma_start(window[32 * q : 32 * q + 4, :].bitcast(I32), rows[4 * q : 4 * q + 4, :])
             return window
 
         def load_table_words(src, width, dtype, name):
@@ -49,8 +51,8 @@ def tile_picked_tokens_plain_two_deltapost_store_plain_kernel(
             nc.sync.dma_start(window[:].bitcast(I32), src.bitcast(I32))
             return window
 
-        def load_weight_words(words, name):
-            raw_words = keep.tile([P, R], I32, name=name + "_raw_words", tag="raw_words")
+        def load_weight_words(words, name, tag):
+            raw_words = keep.tile([P, R], I32, name=name + "_raw_words", tag=tag)
             nc.sync.dma_start(raw_words[:], words[0].rearrange("p c t -> p (c t)").bitcast(I32))
             return raw_words
 
@@ -70,15 +72,16 @@ def tile_picked_tokens_plain_two_deltapost_store_plain_kernel(
             )
 
         token_list = load_list(offs, "token_list")
-        xt_scale_window = load_table_scales(xt_scales, T, "xt_scale_window", nc.gpsimd)
+        xt_scale_window = load_table_scales(xt_scales, T, "xt_scale_window", [nc.gpsimd, nc.vector], nc.scalar)
         w_raw_scales = load_weight_scales(w_scales, "w")
         xt_word_window = load_table_words(xt_words[0], T, U16, "xt_word_window")
-        w_raw_words = load_weight_words(w_words, "w")
+        w_raw_words = load_weight_words(w_words, "w", "w_raw_words")
         put_first_list = load_list(offs3, "put_first_list")
 
         first_boards = [keep.tile([P, C], F32, name="first_board%d" % i) for i in range(2)]
-        for board in first_boards:
-            nc.vector.memset(board[:], 0.0)
+        nc.vector.memset(first_boards[0][:], 0.0)
+        nc.gpsimd.memset(first_boards[1][:, : C // 2], 0.0)
+        nc.vector.memset(first_boards[1][:, C // 2 :], 0.0)
 
         w_dealt_words = keep.tile([P, R], I32, align_bytes=64)
         w_dealt_scales = keep.tile([P, R], U8, align_bytes=64)
@@ -91,35 +94,45 @@ def tile_picked_tokens_plain_two_deltapost_store_plain_kernel(
                 COPY,
             )
 
-        deal(w_dealt_scales, w_raw_scales, 0, 1)
-        for h in range(2):
-            slots = slice(h * HALF, (h + 1) * HALF)
+        def gather_tokens(slots):
             entries = token_list[:, slots.start // 16 : slots.stop // 16]
             token_scales = keep.tile([P, HALF], U8, align_bytes=64)
             token_words = keep.tile([P, HALF], U16, align_bytes=64)
             nc.vector.tensor_copy(token_scales[:], xt_scale_window[:].indirect(entries))
             nc.vector.tensor_copy(token_words[:], xt_word_window[:].indirect(entries))
-            for t in range(PACK):
-                if h == 0 and t < 2:
-                    deal(w_dealt_words, w_raw_words, t, 1 if t == 0 else PACK)
-                if h == 0 and t == 1:
-                    deal(w_dealt_scales, w_raw_scales, 1, PACK)
-                acc = psum.tile([P, J], F32, name="acc", tag="acc")
-                nc.tensor.matmul_mx(
-                    out=acc[:, :HALF],
-                    lhsT=w_dealt_words[:, t * P : (t + 1) * P].bitcast(FP8X4),
-                    lhsT_scale=w_dealt_scales[:, t * P : (t + 1) * P],
-                    rhs=token_words[:].bitcast(FP4X4),
-                    rhs_scale=token_scales[:],
-                    start=True,
-                    stop=True,
-                )
-                if h == 0 and t == 0:
-                    nc.scalar.activation(a_rows[t][:, slots], acc[:, :HALF], COPY)
-                else:
-                    nc.vector.tensor_copy(a_rows[t][:, slots], acc[:, :HALF])
-                if t < 2:
-                    put_first(t, slots)
+            return token_words, token_scales
+
+        def first_product(t, tokens):
+            acc = psum.tile([P, J], F32, name="acc", tag="acc")
+            nc.tensor.matmul_mx(
+                out=acc[:, :HALF],
+                lhsT=w_dealt_words[:, t * P : (t + 1) * P].bitcast(FP8X4),
+                lhsT_scale=w_dealt_scales[:, t * P : (t + 1) * P],
+                rhs=tokens[0][:].bitcast(FP4X4),
+                rhs_scale=tokens[1][:],
+                start=True,
+                stop=True,
+            )
+            return acc[:, :HALF]
+
+        early, late = slice(0, HALF), slice(HALF, J)
+        deal(w_dealt_scales, w_raw_scales, 0, 1)
+        tokens = gather_tokens(early)
+        deal(w_dealt_words, w_raw_words, 0, 1)
+        nc.scalar.activation(a_rows[0][:, early], first_product(0, tokens), COPY)
+        put_first(0, early)
+        deal(w_dealt_scales, w_raw_scales, 1, PACK)
+        deal(w_dealt_words, w_raw_words, 1, PACK)
+        early_products = [first_product(t, tokens) for t in range(1, PACK)]
+        nc.vector.tensor_copy(a_rows[1][:, early], early_products[0])
+        put_first(1, early)
+        tokens = gather_tokens(late)
+        for t in range(PACK):
+            if t >= 2:
+                nc.vector.tensor_copy(a_rows[t][:, early], early_products[t - 1])
+            nc.vector.tensor_copy(a_rows[t][:, late], first_product(t, tokens))
+            if t < 2:
+                put_first(t, late)
         all_slots = slice(0, J)
 
         read_first_list = load_list(offs4, "read_first_list")
@@ -132,10 +145,10 @@ def tile_picked_tokens_plain_two_deltapost_store_plain_kernel(
         nc.sync.dma_start(second_weights[:], sb.rearrange("(p t) o -> p (t o)", t=PACK))
         store_list = load_list(offs7, "store_list")
 
-        xo_scale_window = load_table_scales(xo_scales, M, "xo_scale_window", nc.vector)
+        xo_scale_window = load_table_scales(xo_scales, M, "xo_scale_window", [nc.vector], nc.sync)
         xo_word_window = load_table_words(xo_words[0], M, U16, "xo_word_window")
         w2_raw_scales = load_weight_scales(w2_scales, "w2")
-        w2_raw_words = load_weight_words(w2_words, "w2")
+        w2_raw_words = load_weight_words(w2_words, "w2", "w_raw_words")
         w2_dealt_words = keep.tile([P, R], I32, align_bytes=64)
         w2_dealt_scales = keep.tile([P, R], U8, align_bytes=64)
         deal(w2_dealt_scales, w2_raw_scales, 0, PACK)
@@ -202,7 +215,7 @@ def tile_picked_tokens_plain_two_deltapost_store_plain_kernel(
             if 0 <= step - 3 < PACK:
                 read_second(step - 3)
 
-        vs_scale_window = load_table_scales(vs_scales, S, "vs_scale_window", nc.vector)
+        vs_scale_window = load_table_scales(vs_scales, S, "vs_scale_window", [nc.vector], nc.sync)
         vs_word_window = load_table_words(vs_words[0].rearrange("p c t -> p (c t)"), S, U32, "vs_word_window")
         store_words = keep.tile([P, N], U32, align_bytes=64)
         store_scales = keep.tile([P, N], U8, align_bytes=64)

@@ -36,15 +36,17 @@ def tile_picked_tokens_plain_two_deltapost_store_plain_kernel(
             nc.sync.dma_start(tile[:], src)
             return tile
 
-        def load_table_scales(src, width, name, clears, queue):
+        def clear_scale_window(width, name, clears):
             window = keep.tile([P, width], U8, name=name, tag="scale_window", align_bytes=64)
             share = width // len(clears)
             for i, clear in enumerate(clears):
                 clear.memset(window[:, i * share : (i + 1) * share].bitcast(I32), 0)
+            return window
+
+        def load_scale_rows(window, src):
             rows = src[0].bitcast(I32)
             for q in range(QUADS):
-                queue.dma_start(window[32 * q : 32 * q + 4, :].bitcast(I32), rows[4 * q : 4 * q + 4, :])
-            return window
+                nc.sync.dma_start(window[32 * q : 32 * q + 4, :].bitcast(I32), rows[4 * q : 4 * q + 4, :])
 
         def load_table_words(src, width, dtype, name):
             window = keep.tile([P, width], dtype, name=name, tag="word_window", align_bytes=64)
@@ -52,14 +54,14 @@ def tile_picked_tokens_plain_two_deltapost_store_plain_kernel(
             return window
 
         def load_weight_words(words, name, tag):
-            raw_words = keep.tile([P, R], I32, name=name + "_raw_words", tag=tag)
+            raw_words = keep.tile([P, R], I32, name=name + "_raw_words", tag=tag, align_bytes=64)
             nc.sync.dma_start(raw_words[:], words[0].rearrange("p c t -> p (c t)").bitcast(I32))
             return raw_words
 
-        def load_weight_scales(scales, name):
+        def load_weight_scales(scales, name, tag):
             staged = keep.tile([4, QUADS, R // 4], I32, name=name + "_staged", tag="staged")
             nc.sync.dma_start(staged[:], scales[0].bitcast(I32).rearrange("(q i) n -> i q n", i=4))
-            raw_scales = keep.tile([P, R], U8, name=name + "_raw_scales", tag="raw_scales")
+            raw_scales = keep.tile([P, R], U8, name=name + "_raw_scales", tag=tag, align_bytes=64)
             nc.vector.memset(raw_scales[:].bitcast(I32), 0)
             for q in range(QUADS):
                 nc.vector.tensor_copy(raw_scales[32 * q : 32 * q + 4, :].bitcast(I32), staged[:, q, :])
@@ -72,16 +74,18 @@ def tile_picked_tokens_plain_two_deltapost_store_plain_kernel(
             )
 
         token_list = load_list(offs, "token_list")
-        xt_scale_window = load_table_scales(xt_scales, T, "xt_scale_window", [nc.gpsimd, nc.vector], nc.scalar)
-        w_raw_scales = load_weight_scales(w_scales, "w")
-        xt_word_window = load_table_words(xt_words[0], T, U16, "xt_word_window")
+        xt_scale_window = clear_scale_window(T, "xt_scale_window", [nc.gpsimd, nc.vector])
+        w_raw_scales = load_weight_scales(w_scales, "w", "w_raw_scales")
         w_raw_words = load_weight_words(w_words, "w", "w_raw_words")
+        load_scale_rows(xt_scale_window, xt_scales)
+        xt_word_window = load_table_words(xt_words[0], T, U16, "xt_word_window")
         put_first_list = load_list(offs3, "put_first_list")
 
-        first_boards = [keep.tile([P, C], F32, name="first_board%d" % i) for i in range(2)]
+        first_boards = [keep.tile([P, C], F32, name="first_board%d" % i) for i in range(3)]
         nc.vector.memset(first_boards[0][:], 0.0)
         nc.gpsimd.memset(first_boards[1][:, : C // 2], 0.0)
         nc.vector.memset(first_boards[1][:, C // 2 :], 0.0)
+        nc.gpsimd.memset(first_boards[2][:], 0.0)
 
         w_dealt_words = keep.tile([P, R], I32, align_bytes=64)
         w_dealt_scales = keep.tile([P, R], U8, align_bytes=64)
@@ -89,7 +93,7 @@ def tile_picked_tokens_plain_two_deltapost_store_plain_kernel(
 
         def put_first(t, slots):
             nc.scalar.activation(
-                first_boards[t % 2][:].indirect(put_first_list[:, slots.start // 16 : slots.stop // 16]),
+                first_boards[t % 3][:].indirect(put_first_list[:, slots.start // 16 : slots.stop // 16]),
                 a_rows[t][:, slots],
                 COPY,
             )
@@ -116,22 +120,21 @@ def tile_picked_tokens_plain_two_deltapost_store_plain_kernel(
             return acc[:, :HALF]
 
         early, late = slice(0, HALF), slice(HALF, J)
-        deal(w_dealt_scales, w_raw_scales, 0, 1)
+        deal(w_dealt_scales, w_raw_scales, 0, PACK)
+        deal(w_dealt_words, w_raw_words, 0, PACK)
         tokens = gather_tokens(early)
-        deal(w_dealt_words, w_raw_words, 0, 1)
         nc.scalar.activation(a_rows[0][:, early], first_product(0, tokens), COPY)
         put_first(0, early)
-        deal(w_dealt_scales, w_raw_scales, 1, PACK)
-        deal(w_dealt_words, w_raw_words, 1, PACK)
         early_products = [first_product(t, tokens) for t in range(1, PACK)]
-        nc.vector.tensor_copy(a_rows[1][:, early], early_products[0])
-        put_first(1, early)
+        for t in (1, 2):
+            nc.vector.tensor_copy(a_rows[t][:, early], early_products[t - 1])
+            put_first(t, early)
         tokens = gather_tokens(late)
         for t in range(PACK):
-            if t >= 2:
+            if t == 3:
                 nc.vector.tensor_copy(a_rows[t][:, early], early_products[t - 1])
             nc.vector.tensor_copy(a_rows[t][:, late], first_product(t, tokens))
-            if t < 2:
+            if t < 3:
                 put_first(t, late)
         all_slots = slice(0, J)
 
@@ -145,10 +148,11 @@ def tile_picked_tokens_plain_two_deltapost_store_plain_kernel(
         nc.sync.dma_start(second_weights[:], sb.rearrange("(p t) o -> p (t o)", t=PACK))
         store_list = load_list(offs7, "store_list")
 
-        xo_scale_window = load_table_scales(xo_scales, M, "xo_scale_window", [nc.vector], nc.sync)
+        xo_scale_window = clear_scale_window(M, "xo_scale_window", [nc.vector])
+        load_scale_rows(xo_scale_window, xo_scales)
         xo_word_window = load_table_words(xo_words[0], M, U16, "xo_word_window")
-        w2_raw_scales = load_weight_scales(w2_scales, "w2")
-        w2_raw_words = load_weight_words(w2_words, "w2", "w_raw_words")
+        w2_raw_scales = load_weight_scales(w2_scales, "w2", "token_scales")
+        w2_raw_words = load_weight_words(w2_words, "w2", "token_words")
         w2_dealt_words = keep.tile([P, R], I32, align_bytes=64)
         w2_dealt_scales = keep.tile([P, R], U8, align_bytes=64)
         deal(w2_dealt_scales, w2_raw_scales, 0, PACK)
@@ -179,7 +183,7 @@ def tile_picked_tokens_plain_two_deltapost_store_plain_kernel(
 
         def read_first(t):
             nc.scalar.activation(
-                taken[t][:], first_boards[t % 2][:].indirect(read_first_list[:]), COPY,
+                taken[t][:], first_boards[t % 3][:].indirect(read_first_list[:]), COPY,
                 scale=first_weights[:, t : t + 1],
             )
             nc.vector.tensor_tensor(difference[t][:], b_rows[t][:], taken[t][:], SUBTRACT)
@@ -206,7 +210,7 @@ def tile_picked_tokens_plain_two_deltapost_store_plain_kernel(
                 )
 
         for step in range(1, PACK + 3):
-            if 2 <= step < PACK:
+            if step == 3:
                 put_first(step, all_slots)
             if step - 1 < PACK:
                 read_first(step - 1)
@@ -215,7 +219,8 @@ def tile_picked_tokens_plain_two_deltapost_store_plain_kernel(
             if 0 <= step - 3 < PACK:
                 read_second(step - 3)
 
-        vs_scale_window = load_table_scales(vs_scales, S, "vs_scale_window", [nc.vector], nc.sync)
+        vs_scale_window = clear_scale_window(S, "vs_scale_window", [nc.vector])
+        load_scale_rows(vs_scale_window, vs_scales)
         vs_word_window = load_table_words(vs_words[0].rearrange("p c t -> p (c t)"), S, U32, "vs_word_window")
         store_words = keep.tile([P, N], U32, align_bytes=64)
         store_scales = keep.tile([P, N], U8, align_bytes=64)
@@ -226,11 +231,12 @@ def tile_picked_tokens_plain_two_deltapost_store_plain_kernel(
             hid_words = keep.tile([P, P], U32, name="hid_words%d" % g, align_bytes=64)
             hid_scales = keep.tile([P, P], U8, name="hid_scales%d" % g, align_bytes=64)
             nc.vector.quantize_mx(out=hid_words[:].bitcast(FP8X4), scales=hid_scales[:], in_=hid_grouped[g][:])
-            y_acc = psum.tile([P, J], F32, name="y_acc", tag="acc")
+            y_rows = keep.tile([P, N], F32, name="y_rows%d" % g)
             for half in range(N // P):
                 features = slice(half * P, (half + 1) * P)
+                y_acc = psum.tile([P, J], F32, name="y_acc", tag="acc")
                 nc.tensor.matmul_mx(
-                    out=y_acc[:, features],
+                    out=y_acc[:, :P],
                     lhsT=store_words[:, features].bitcast(FP8X4),
                     lhsT_scale=store_scales[:, features],
                     rhs=hid_words[:].bitcast(FP8X4),
@@ -238,11 +244,10 @@ def tile_picked_tokens_plain_two_deltapost_store_plain_kernel(
                     start=True,
                     stop=True,
                 )
-            y_rows = keep.tile([P, N], F32, name="y_rows%d" % g)
-            if g == 0:
-                nc.scalar.copy(y_rows[:], y_acc[:, :N])
-            else:
-                nc.vector.tensor_copy(y_rows[:], y_acc[:, :N])
+                if half == 0:
+                    nc.scalar.copy(y_rows[:, features], y_acc[:, :P])
+                else:
+                    nc.vector.tensor_copy(y_rows[:, features], y_acc[:, :P])
             nc.sync.dma_start(
                 out.rearrange("(h p) o -> p h o", p=P)[:, :, g * P : (g + 1) * P],
                 y_rows[:].rearrange("p (h o) -> p h o", o=P),

@@ -67,10 +67,10 @@ def tile_picked_tokens_plain_two_deltapost_store_plain_kernel(
                 nc.vector.tensor_copy(raw_scales[32 * q : 32 * q + 4, :].bitcast(I32), staged[:, q, :])
             return raw_scales
 
-        def deal(dealt, raw, first, last):
+        def deal(dealt, raw):
             nc.vector.tensor_copy(
-                dealt[:, first * P : last * P].rearrange("p (t m) -> p t m", m=P),
-                raw[:].rearrange("p (m t) -> p t m", t=PACK)[:, first:last, :],
+                dealt[:].rearrange("p (t m) -> p m t", t=PACK),
+                raw[:].rearrange("p (m t) -> p m t", t=PACK),
             )
 
         token_list = load_list(offs, "token_list")
@@ -81,11 +81,9 @@ def tile_picked_tokens_plain_two_deltapost_store_plain_kernel(
         xt_word_window = load_table_words(xt_words[0], T, U16, "xt_word_window")
         put_first_list = load_list(offs3, "put_first_list")
 
-        first_boards = [keep.tile([P, C], F32, name="first_board%d" % i) for i in range(3)]
-        nc.vector.memset(first_boards[0][:], 0.0)
-        nc.gpsimd.memset(first_boards[1][:, : C // 2], 0.0)
-        nc.vector.memset(first_boards[1][:, C // 2 :], 0.0)
-        nc.gpsimd.memset(first_boards[2][:], 0.0)
+        first_boards = [keep.tile([P, C], F32, name="first_board%d" % i) for i in range(2)]
+        for board in first_boards:
+            nc.vector.memset(board[:], 0.0)
 
         w_dealt_words = keep.tile([P, R], I32, align_bytes=64)
         w_dealt_scales = keep.tile([P, R], U8, align_bytes=64)
@@ -93,7 +91,7 @@ def tile_picked_tokens_plain_two_deltapost_store_plain_kernel(
 
         def put_first(t, slots):
             nc.scalar.activation(
-                first_boards[t % 3][:].indirect(put_first_list[:, slots.start // 16 : slots.stop // 16]),
+                first_boards[t % 2][:].indirect(put_first_list[:, slots.start // 16 : slots.stop // 16]),
                 a_rows[t][:, slots],
                 COPY,
             )
@@ -120,21 +118,20 @@ def tile_picked_tokens_plain_two_deltapost_store_plain_kernel(
             return acc[:, :HALF]
 
         early, late = slice(0, HALF), slice(HALF, J)
-        deal(w_dealt_scales, w_raw_scales, 0, PACK)
-        deal(w_dealt_words, w_raw_words, 0, PACK)
+        deal(w_dealt_scales, w_raw_scales)
+        deal(w_dealt_words, w_raw_words)
         tokens = gather_tokens(early)
         nc.scalar.activation(a_rows[0][:, early], first_product(0, tokens), COPY)
         put_first(0, early)
         early_products = [first_product(t, tokens) for t in range(1, PACK)]
-        for t in (1, 2):
-            nc.vector.tensor_copy(a_rows[t][:, early], early_products[t - 1])
-            put_first(t, early)
+        nc.vector.tensor_copy(a_rows[1][:, early], early_products[0])
+        put_first(1, early)
         tokens = gather_tokens(late)
         for t in range(PACK):
-            if t == 3:
+            if t >= 2:
                 nc.vector.tensor_copy(a_rows[t][:, early], early_products[t - 1])
             nc.vector.tensor_copy(a_rows[t][:, late], first_product(t, tokens))
-            if t < 3:
+            if t < 2:
                 put_first(t, late)
         all_slots = slice(0, J)
 
@@ -155,8 +152,8 @@ def tile_picked_tokens_plain_two_deltapost_store_plain_kernel(
         w2_raw_words = load_weight_words(w2_words, "w2", "token_words")
         w2_dealt_words = keep.tile([P, R], I32, align_bytes=64)
         w2_dealt_scales = keep.tile([P, R], U8, align_bytes=64)
-        deal(w2_dealt_scales, w2_raw_scales, 0, PACK)
-        deal(w2_dealt_words, w2_raw_words, 0, PACK)
+        deal(w2_dealt_scales, w2_raw_scales)
+        deal(w2_dealt_words, w2_raw_words)
         note_words = keep.tile([P, J], U16, align_bytes=64)
         note_scales = keep.tile([P, J], U8, align_bytes=64)
         nc.vector.tensor_copy(note_scales[:], xo_scale_window[:].indirect(note_list[:]))
@@ -183,7 +180,7 @@ def tile_picked_tokens_plain_two_deltapost_store_plain_kernel(
 
         def read_first(t):
             nc.scalar.activation(
-                taken[t][:], first_boards[t % 3][:].indirect(read_first_list[:]), COPY,
+                taken[t][:], first_boards[t % 2][:].indirect(read_first_list[:]), COPY,
                 scale=first_weights[:, t : t + 1],
             )
             nc.vector.tensor_tensor(difference[t][:], b_rows[t][:], taken[t][:], SUBTRACT)
@@ -210,7 +207,7 @@ def tile_picked_tokens_plain_two_deltapost_store_plain_kernel(
                 )
 
         for step in range(1, PACK + 3):
-            if step == 3:
+            if 2 <= step < PACK:
                 put_first(step, all_slots)
             if step - 1 < PACK:
                 read_first(step - 1)

from contextlib import ExitStack

import concourse.mybir as mybir

K, J, R, T, M, O, C, N, S = 512, 512, 512, 2048, 1024, 256, 1024, 256, 1024
FLOPS = 2 * (K * R * J + K * R * J + R * N * O)

F32 = mybir.dt.float32
BF16 = mybir.dt.bfloat16
I32 = mybir.dt.int32
U32 = mybir.dt.uint32
U16 = mybir.dt.uint16
U8 = mybir.dt.uint8
FP8X4 = mybir.dt.float8_e4m3fn_x4
FP4X4 = mybir.dt.float4_e2m1fn_x4
COPY = mybir.ActivationFunctionType.Copy
SUBTRACT = mybir.AluOpType.subtract

P = 128
PACK = 4
QUADS = 4
HALF = J // 2


def tile_picked_tokens_plain_two_deltapost_store_plain_kernel(
    tc, xt_words, xt_scales, w_words, w_scales, xo_words, xo_scales, w2_words, w2_scales,
    sa, sb, vs_words, vs_scales, offs, offs2, offs3, offs4, offs5, offs6, offs7, out,
):
    nc = tc.nc
    with ExitStack() as ctx:
        keep = ctx.enter_context(tc.tile_pool(name="keep", bufs=1))
        psum = ctx.enter_context(tc.psum_pool(name="psum", bufs=4))

        def load_list(src, name):
            tile = keep.tile(list(src.shape), U16, name=name)
            nc.sync.dma_start(tile[:], src)
            return tile

        def clear_scale_window(width, name, clears):
            window = keep.tile([P, width], U8, name=name, tag="scale_window", align_bytes=64)
            share = width // len(clears)
            for i, clear in enumerate(clears):
                clear.memset(window[:, i * share : (i + 1) * share].bitcast(I32), 0)
            return window

        def load_scale_rows(window, src):
            rows = src[0].bitcast(I32)
            for q in range(QUADS):
                nc.sync.dma_start(window[32 * q : 32 * q + 4, :].bitcast(I32), rows[4 * q : 4 * q + 4, :])

        def load_table_words(src, width, dtype, name):
            window = keep.tile([P, width], dtype, name=name, tag="word_window", align_bytes=64)
            nc.sync.dma_start(window[:].bitcast(I32), src.bitcast(I32))
            return window

        def load_weight_words(words, name, tag):
            raw_words = keep.tile([P, R], I32, name=name + "_raw_words", tag=tag, align_bytes=64)
            nc.sync.dma_start(raw_words[:], words[0].rearrange("p c t -> p (c t)").bitcast(I32))
            return raw_words

        def load_weight_scales(scales, name, tag):
            staged = keep.tile([4, QUADS, R // 4], I32, name=name + "_staged", tag="staged")
            nc.sync.dma_start(staged[:], scales[0].bitcast(I32).rearrange("(q i) n -> i q n", i=4))
            raw_scales = keep.tile([P, R], U8, name=name + "_raw_scales", tag=tag, align_bytes=64)
            nc.vector.memset(raw_scales[:].bitcast(I32), 0)
            for q in range(QUADS):
                nc.vector.tensor_copy(raw_scales[32 * q : 32 * q + 4, :].bitcast(I32), staged[:, q, :])
            return raw_scales

        def deal(dealt, raw):
            nc.vector.tensor_copy(
                dealt[:].rearrange("p (t m) -> p m t", t=PACK),
                raw[:].rearrange("p (m t) -> p m t", t=PACK),
            )

        token_list = load_list(offs, "token_list")
        xt_scale_window = clear_scale_window(T, "xt_scale_window", [nc.gpsimd, nc.vector])
        w_raw_scales = load_weight_scales(w_scales, "w", "w_raw_scales")
        w_raw_words = load_weight_words(w_words, "w", "w_raw_words")
        load_scale_rows(xt_scale_window, xt_scales)
        xt_word_window = load_table_words(xt_words[0], T, U16, "xt_word_window")
        put_first_list = load_list(offs3, "put_first_list")

        first_boards = [keep.tile([P, C], F32, name="first_board%d" % i) for i in range(2)]
        for board in first_boards:
            nc.vector.memset(board[:], 0.0)

        w_dealt_words = keep.tile([P, R], I32, align_bytes=64)
        w_dealt_scales = keep.tile([P, R], U8, align_bytes=64)
        a_rows = [keep.tile([P, J], F32, name="a_rows%d" % t, tag="rows%d" % t) for t in range(PACK)]

        def put_first(t, slots):
            nc.scalar.activation(
                first_boards[t % 2][:].indirect(put_first_list[:, slots.start // 16 : slots.stop // 16]),
                a_rows[t][:, slots],
                COPY,
            )

        def gather_tokens(slots):
            entries = token_list[:, slots.start // 16 : slots.stop // 16]
            token_scales = keep.tile([P, HALF], U8, align_bytes=64)
            token_words = keep.tile([P, HALF], U16, align_bytes=64)
            nc.vector.tensor_copy(token_scales[:], xt_scale_window[:].indirect(entries))
            nc.vector.tensor_copy(token_words[:], xt_word_window[:].indirect(entries))
            return token_words, token_scales

        def first_product(t, tokens):
            acc = psum.tile([P, J], F32, name="acc", tag="acc")
            nc.tensor.matmul_mx(
                out=acc[:, :HALF],
                lhsT=w_dealt_words[:, t * P : (t + 1) * P].bitcast(FP8X4),
                lhsT_scale=w_dealt_scales[:, t * P : (t + 1) * P],
                rhs=tokens[0][:].bitcast(FP4X4),
                rhs_scale=tokens[1][:],
                start=True,
                stop=True,
            )
            return acc[:, :HALF]

        early, late = slice(0, HALF), slice(HALF, J)
        deal(w_dealt_scales, w_raw_scales)
        deal(w_dealt_words, w_raw_words)
        tokens = gather_tokens(early)
        nc.scalar.activation(a_rows[0][:, early], first_product(0, tokens), COPY)
        put_first(0, early)
        early_products = [first_product(t, tokens) for t in range(1, PACK)]
        nc.vector.tensor_copy(a_rows[1][:, early], early_products[0])
        put_first(1, early)
        tokens = gather_tokens(late)
        for t in range(PACK):
            if t >= 2:
                nc.vector.tensor_copy(a_rows[t][:, early], early_products[t - 1])
            nc.vector.tensor_copy(a_rows[t][:, late], first_product(t, tokens))
            if t < 2:
                put_first(t, late)
        all_slots = slice(0, J)

        read_first_list = load_list(offs4, "read_first_list")
        first_weights = keep.tile([P, PACK], F32)
        nc.sync.dma_start(first_weights[:], sa.rearrange("(p t) o -> p (t o)", t=PACK))
        note_list = load_list(offs2, "note_list")
        put_second_list = load_list(offs5, "put_second_list")
        read_second_list = load_list(offs6, "read_second_list")
        second_weights = keep.tile([P, PACK], F32)
        nc.sync.dma_start(second_weights[:], sb.rearrange("(p t) o -> p (t o)", t=PACK))
        store_list = load_list(offs7, "store_list")

        xo_scale_window = clear_scale_window(M, "xo_scale_window", [nc.vector])
        load_scale_rows(xo_scale_window, xo_scales)
        xo_word_window = load_table_words(xo_words[0], M, U16, "xo_word_window")
        w2_raw_scales = load_weight_scales(w2_scales, "w2", "token_scales")
        w2_raw_words = load_weight_words(w2_words, "w2", "token_words")
        w2_dealt_words = keep.tile([P, R], I32, align_bytes=64)
        w2_dealt_scales = keep.tile([P, R], U8, align_bytes=64)
        deal(w2_dealt_scales, w2_raw_scales)
        deal(w2_dealt_words, w2_raw_words)
        note_words = keep.tile([P, J], U16, align_bytes=64)
        note_scales = keep.tile([P, J], U8, align_bytes=64)
        nc.vector.tensor_copy(note_scales[:], xo_scale_window[:].indirect(note_list[:]))
        nc.vector.tensor_copy(note_words[:], xo_word_window[:].indirect(note_list[:]))
        b_rows = []
        for t in range(PACK):
            b_acc = psum.tile([P, J], F32, name="b_acc", tag="b_acc")
            nc.tensor.matmul_mx(
                out=b_acc[:],
                lhsT=w2_dealt_words[:, t * P : (t + 1) * P].bitcast(FP8X4),
                lhsT_scale=w2_dealt_scales[:, t * P : (t + 1) * P],
                rhs=note_words[:].bitcast(FP4X4),
                rhs_scale=note_scales[:],
                start=True,
                stop=True,
            )
            b_rows.append(b_acc)

        taken = [keep.tile([P, J], F32, name="taken%d" % t) for t in range(PACK)]
        difference = [keep.tile([P, J], F32, name="difference%d" % t) for t in range(PACK)]
        positive = [keep.tile([P, J], F32, name="positive%d" % t) for t in range(PACK)]
        hid_rows = keep.tile([P, PACK * O], BF16, align_bytes=64)
        hid_grouped = [keep.tile([P, P * PACK], BF16, name="hid_grouped%d" % g, align_bytes=64) for g in range(2)]

        def read_first(t):
            nc.scalar.activation(
                taken[t][:], first_boards[t % 2][:].indirect(read_first_list[:]), COPY,
                scale=first_weights[:, t : t + 1],
            )
            nc.vector.tensor_tensor(difference[t][:], b_rows[t][:], taken[t][:], SUBTRACT)
            nc.vector.tensor_scalar_max(positive[t][:], difference[t][:], 0.0)

        second_boards = []

        def put_second(t):
            if t < 2:
                board = keep.tile([P, C], F32, name="second_board%d" % t, tag="rows%d" % t)
                nc.vector.memset(board[:], 0.0)
                second_boards.append(board)
            nc.scalar.activation(second_boards[t % 2][:].indirect(put_second_list[:]), positive[t][:], COPY)

        def read_second(t):
            nc.scalar.activation(
                hid_rows[:, t * O : (t + 1) * O], second_boards[t % 2][:].indirect(read_second_list[:]), COPY,
                scale=second_weights[:, t : t + 1],
            )
            for g in range(2):
                nc.vector.tensor_copy(
                    hid_grouped[g][:].rearrange("p (o t) -> p o t", t=PACK)[:, :, t],
                    hid_rows[:, t * O + g * P : t * O + (g + 1) * P],
                )

        for step in range(1, PACK + 3):
            if 2 <= step < PACK:
                put_first(step, all_slots)
            if step - 1 < PACK:
                read_first(step - 1)
            if 0 <= step - 2 < PACK:
                put_second(step - 2)
            if 0 <= step - 3 < PACK:
                read_second(step - 3)

        vs_scale_window = clear_scale_window(S, "vs_scale_window", [nc.vector])
        load_scale_rows(vs_scale_window, vs_scales)
        vs_word_window = load_table_words(vs_words[0].rearrange("p c t -> p (c t)"), S, U32, "vs_word_window")
        store_words = keep.tile([P, N], U32, align_bytes=64)
        store_scales = keep.tile([P, N], U8, align_bytes=64)
        nc.vector.tensor_copy(store_scales[:], vs_scale_window[:].indirect(store_list[:]))
        nc.vector.tensor_copy(store_words[:], vs_word_window[:].indirect(store_list[:]))

        for g in range(2):
            hid_words = keep.tile([P, P], U32, name="hid_words%d" % g, align_bytes=64)
            hid_scales = keep.tile([P, P], U8, name="hid_scales%d" % g, align_bytes=64)
            nc.vector.quantize_mx(out=hid_words[:].bitcast(FP8X4), scales=hid_scales[:], in_=hid_grouped[g][:])
            y_rows = keep.tile([P, N], F32, name="y_rows%d" % g)
            for half in range(N // P):
                features = slice(half * P, (half + 1) * P)
                y_acc = psum.tile([P, J], F32, name="y_acc", tag="acc")
                nc.tensor.matmul_mx(
                    out=y_acc[:, :P],
                    lhsT=store_words[:, features].bitcast(FP8X4),
                    lhsT_scale=store_scales[:, features],
                    rhs=hid_words[:].bitcast(FP8X4),
                    rhs_scale=hid_scales[:],
                    start=True,
                    stop=True,
                )
                if half == 0:
                    nc.scalar.copy(y_rows[:, features], y_acc[:, :P])
                else:
                    nc.vector.tensor_copy(y_rows[:, features], y_acc[:, :P])
            nc.sync.dma_start(
                out.rearrange("(h p) o -> p h o", p=P)[:, :, g * P : (g + 1) * P],
                y_rows[:].rearrange("p (h o) -> p h o", o=P),
            )
